import numpy as np
import ml_dtypes


def mxq(x, axis, fmt="e4m3"):
    dtype, down = {"e4m3": (ml_dtypes.float8_e4m3fn, 7), "e5m2": (ml_dtypes.float8_e5m2, 14)}[fmt]
    v = np.moveaxis(np.asarray(x, np.float32).astype(ml_dtypes.bfloat16).astype(np.float64), axis, -1)
    blocks = v.reshape(v.shape[:-1] + (-1, 32))
    amax = np.abs(blocks).max(-1, keepdims=True)
    byte = np.maximum(np.where(amax > 0, np.frexp(amax)[1] - 1 + 127, 0) - down, 1)
    scale = np.exp2(byte - 127.0)
    codes = (blocks / scale).astype(np.float32).astype(dtype).astype(np.float64)
    return np.moveaxis((codes * scale).reshape(v.shape), -1, axis)


WIDE = False


def mx_kscale(k):
    if not WIDE:
        return np.ones(k)
    levels = np.array([10, -10, 5, -5, 0])
    if k % 512:
        return np.exp2(np.random.permutation(np.resize(levels, k // 32))).repeat(32)
    a = np.empty((k // 512, 16))
    for p in range(k // 512):
        a[p, :8] = np.random.permutation(np.resize(levels, 8))
        for g in range(8):
            far = levels[np.abs(levels - a[p, g]) >= 10]
            a[p, g + 8] = far[np.random.randint(len(far))]
    return np.exp2(a.ravel()).repeat(32)


def f64(x):
    return np.asarray(x).astype(np.float64)


def striped(idx):
    return np.tile(idx.reshape(-1, 16).T, (8, 1)).astype(np.uint16)


def unstriped(offs):
    return offs[:16].T.reshape(-1).astype(np.int64)


def pack_weight(w):
    k, n = w.shape
    w = f64(np.asarray(w, np.float32).astype(ml_dtypes.bfloat16)).reshape(k // 32, 32, n)
    amax = np.abs(w).max(1)
    byte = np.clip(np.where(amax > 0, np.frexp(amax)[1] - 1 + 127 - 7, 1), 1, 254)
    scaled = (w * np.exp2(127.0 - byte)[:, None, :]).reshape(k, n).astype(np.float32)
    words = np.ascontiguousarray(scaled.reshape(k // 512, 128, 4, n).transpose(0, 1, 3, 2)).astype(ml_dtypes.float8_e4m3fn).view(np.uint8)
    return words, np.ascontiguousarray(byte.astype(np.uint8).reshape(k // 512, 16, n))


def unpack_weight(words, scales):
    g, p, n, _ = words.shape
    vals = np.ascontiguousarray(words).view(ml_dtypes.float8_e4m3fn).astype(np.float64) * np.repeat(np.exp2(scales.astype(np.float64) - 127.0), 8, axis=1)[..., None]
    return vals.transpose(0, 1, 3, 2).reshape(g * 512, n)


K, T, S, V, R = 512, 1024, 512, 512, 256
P = 2 ** 7


def setup_inputs():
    n = np.random.standard_normal
    s = mx_kscale(K)[:, None]
    packed_xT = pack_weight(n((K, T)) * s)
    return {
        "x_words": packed_xT[0],
        "x_scales": packed_xT[1],
        "hT": (n((K, V)) / np.sqrt(K) / s).astype(np.float32),
        "share": (np.tile(np.random.uniform(0.1, 0.9, R), (P, 1))).astype(np.float32),
        "inv": (np.tile(np.random.uniform(1.0, 1.4, R), (P, 1))).astype(np.float32),
        "offs": striped(np.random.permutation(T)[:S]),
        "one": striped(np.random.permutation(S)[:R]),
        "two": striped(np.random.permutation(S)[:R]),
    }


def reference(x_words, x_scales, hT, share, inv, offs, one, two):
    hTq = mxq(f64(hT), 0, "e4m3")
    xq = unpack_weight(x_words, x_scales)[:, unstriped(offs)]
    y = hTq.T @ xq
    p2 = y[:, unstriped(two)]
    syn = (p2 + f64(share)[:1] * (y[:, unstriped(one)] - p2)) * f64(inv)[:1]
    al = np.concatenate([y, syn], axis=1)
    ex = np.exp(al)
    lse = np.log(ex.sum(axis=1, keepdims=True))
    return al - lse

@@ -1,0 +1,144 @@
+from contextlib import ExitStack
+
+import concourse.mybir as mybir
+
+K, T, S, V, R = 512, 1024, 512, 512, 256
+P = 128
+PACK = 4
+BLOCKS = V // P
+W = S + R
+ROOT = 64
+TERMS = 11
+FLOPS = 2 * K * V * S
+
+F32 = mybir.dt.float32
+BF16 = mybir.dt.bfloat16
+I32 = mybir.dt.int32
+U32 = mybir.dt.uint32
+U16 = mybir.dt.uint16
+U8 = mybir.dt.uint8
+FP8X4 = mybir.dt.float8_e4m3fn_x4
+ALU = mybir.AluOpType
+ACT = mybir.ActivationFunctionType
+AXIS = mybir.AxisListType
+
+
+def tile_picked_ymochi_log_p_kernel(tc, x_words, x_scales, hT, share, inv, offs, one, two, out):
+    nc = tc.nc
+    with ExitStack() as ctx:
+        keep = ctx.enter_context(tc.tile_pool(name="keep", bufs=1))
+        psum = ctx.enter_context(tc.psum_pool(name="psum", bufs=1))
+
+        offs_sb = keep.tile([P, S // 16], U16)
+        one_sb = keep.tile([P, R // 16], U16)
+        two_sb = keep.tile([P, R // 16], U16)
+        words = keep.tile([P, T], I32)
+        scale_rows = keep.tile([P, T], U8)
+        share_sb = keep.tile([P, R], F32)
+        inv_sb = keep.tile([P, R], F32)
+        h_raw = [keep.tile([P, PACK, P], F32, name=f"h_raw{b}") for b in range(BLOCKS)]
+        h_view = hT.rearrange("(p j) t -> p j t", j=PACK)
+
+        nc.gpsimd.memset(scale_rows[:].bitcast(I32), 0)
+        nc.sync.dma_start(offs_sb[:], offs)
+        for q in range(4):
+            nc.sync.dma_start(
+                out=scale_rows[32 * q : 32 * q + 4, :].bitcast(I32),
+                in_=x_scales[0, 4 * q : 4 * q + 4, :].bitcast(I32),
+            )
+        nc.sync.dma_start(out=h_raw[0][:], in_=h_view[:, :, 0:P])
+        nc.sync.dma_start(out=words[:], in_=x_words[0].rearrange("p n t -> p (n t)").bitcast(I32))
+        nc.sync.dma_start(out=h_raw[1][:], in_=h_view[:, :, P : 2 * P])
+        nc.sync.dma_start(share_sb[:], share)
+        nc.sync.dma_start(inv_sb[:], inv)
+        nc.sync.dma_start(one_sb[:], one)
+        nc.sync.dma_start(two_sb[:], two)
+        for b in range(2, BLOCKS):
+            nc.sync.dma_start(out=h_raw[b][:], in_=h_view[:, :, b * P : (b + 1) * P])
+
+        counts = keep.tile([P, BLOCKS, TERMS], F32)
+        horner = keep.tile([P, BLOCKS, TERMS + 1], F32)
+        exponent = keep.tile([P, 1], F32)
+        nc.gpsimd.iota(counts[:], pattern=[[0, BLOCKS], [-1, TERMS]], base=TERMS, channel_multiplier=0, allow_small_or_imprecise_dtypes=True)
+        nc.gpsimd.memset(exponent[:], -1.0 / ROOT)
+        nc.vector.tensor_scalar(counts[:], counts[:], -1.0 / ROOT, None, op0=ALU.mult)
+        nc.vector.reciprocal(horner[:, :, 0:TERMS], counts[:])
+
+        x_codes = keep.tile([P, S], U32, align_bytes=64)
+        x_bytes = keep.tile([P, S], U8, align_bytes=64)
+        nc.vector.tensor_copy(x_bytes[:], scale_rows[:].indirect(offs_sb[:]))
+        nc.vector.tensor_copy(x_codes[:], words[:].bitcast(U32).indirect(offs_sb[:]))
+
+        scores = []
+        for b in range(BLOCKS):
+            grouped = keep.tile([P, P, PACK], BF16, name=f"grouped{b}", align_bytes=64)
+            nc.scalar.activation(
+                grouped[:].rearrange("p (c i) j -> p c j i", i=4),
+                h_raw[b][:].rearrange("p j (c i) -> p c j i", i=4),
+                ACT.Copy,
+            )
+            h_codes = keep.tile([P, P], U32, name=f"h_codes{b}", align_bytes=64)
+            h_bytes = keep.tile([P, P], U8, name=f"h_bytes{b}", align_bytes=64)
+            nc.vector.quantize_mx(out=h_codes[:].bitcast(FP8X4), scales=h_bytes[:], in_=grouped[:].rearrange("p t j -> p (t j)"))
+            acc = psum.tile([P, S], F32, name=f"acc{b}")
+            nc.tensor.matmul_mx(
+                out=acc[:], lhsT=h_codes[:].bitcast(FP8X4), lhsT_scale=h_bytes[:],
+                rhs=x_codes[:].bitcast(FP8X4), rhs_scale=x_bytes[:], start=True, stop=True,
+            )
+            scores.append(acc)
+
+        weight_one = keep.tile([P, R], F32)
+        weight_two = keep.tile([P, R], F32)
+        nc.vector.tensor_tensor(weight_one[:], share_sb[:], inv_sb[:], ALU.mult)
+        nc.vector.tensor_tensor(weight_two[:], inv_sb[:], weight_one[:], ALU.subtract)
+
+        logits = [keep.tile([P, W + 1], F32, name=f"logits{b}") for b in range(BLOCKS)]
+        part_one = [keep.tile([P, R], F32, name=f"part_one{b}") for b in range(BLOCKS)]
+        part_two = [keep.tile([P, R], F32, name=f"part_two{b}") for b in range(BLOCKS)]
+        result = [keep.tile([P, W], F32, name=f"result{b}") for b in range(BLOCKS)]
+        total = [keep.tile([P, 1], F32, name=f"total{b}") for b in range(BLOCKS)]
+        root = [keep.tile([P, 1], F32, name=f"root{b}") for b in range(BLOCKS)]
+        gap = [keep.tile([P, 1], F32, name=f"gap{b}") for b in range(BLOCKS)]
+        series = [keep.tile([P, TERMS + 1], F32, name=f"series{b}") for b in range(BLOCKS)]
+
+        def leave_psum(b):
+            nc.vector.tensor_scalar(logits[b][:, 0:S], scores[b][:], 1.0, None, op0=ALU.mult, op1=ALU.max, accum_out=logits[b][:, W : W + 1])
+
+        def gather_one(b):
+            nc.vector.tensor_tensor(part_one[b][:], logits[b][:].indirect(one_sb[:]), weight_one[:], ALU.mult)
+
+        def gather_two(b):
+            nc.vector.tensor_tensor(part_two[b][:], logits[b][:].indirect(two_sb[:]), weight_two[:], ALU.mult)
+
+        def mix(b):
+            nc.vector.tensor_tensor(logits[b][:, S:W], part_one[b][:], part_two[b][:], ALU.add)
+
+        def row_max(b):
+            nc.vector.tensor_reduce(horner[:, b, TERMS : TERMS + 1], logits[b][:, S : W + 1], axis=AXIS.X, op=ALU.max, negate=True)
+            nc.scalar.activation(result[b][:], logits[b][:, 0:W], ACT.Exp, bias=horner[:, b, TERMS : TERMS + 1], accum_out=total[b][:])
+            nc.gpsimd.tensor_tensor(root[b][:], total[b][:], exponent[:], ALU.pow)
+            nc.gpsimd.tensor_scalar(gap[b][:], root[b][:], -1.0, 1.0, op0=ALU.mult, op1=ALU.add)
+
+        def finish(b):
+            nc.vector.tensor_tensor_scan(series[b][:], gap[b][:].to_broadcast([P, TERMS + 1]), horner[:, b, :], 0.0, op0=ALU.mult, op1=ALU.add)
+            minus_lse = series[b][:, TERMS : TERMS + 1]
+            if b < BLOCKS - 1:
+                nc.scalar.activation(result[b][:], logits[b][:, 0:W], ACT.Identity, bias=minus_lse)
+            else:
+                nc.vector.tensor_scalar(result[b][:, 0:S], logits[b][:, 0:S], minus_lse, None, op0=ALU.add)
+                nc.scalar.activation(result[b][:, S:W], logits[b][:, S:W], ACT.Identity, bias=minus_lse)
+            nc.sync.dma_start(out=out[b * P : (b + 1) * P, :], in_=result[b][:])
+
+        leave_psum(0)
+        gather_one(0)
+        for b in range(BLOCKS):
+            gather_two(b)
+            if b + 1 < BLOCKS:
+                leave_psum(b + 1)
+            mix(b)
+            if b + 1 < BLOCKS:
+                gather_one(b + 1)
+            row_max(b)
+            if b > 0:
+                finish(b - 1)
+        finish(BLOCKS - 1)

@@ -1,3 +1,4 @@
+import math
 from contextlib import ExitStack
 
 import concourse.mybir as mybir
@@ -7,8 +8,8 @@ P = 128
 PACK = 4
 BLOCKS = V // P
 W = S + R
-ROOT = 64
-TERMS = 11
+STEP = 0.4
+FIRST_NODE, NODES = -71, 80
 FLOPS = 2 * K * V * S
 
 F32 = mybir.dt.float32
@@ -36,7 +37,10 @@ def tile_picked_ymochi_log_p_kernel(tc, x_words, x_scales, hT, share, inv, offs,
         scale_rows = keep.tile([P, T], U8)
         share_sb = keep.tile([P, R], F32)
         inv_sb = keep.tile([P, R], F32)
-        h_raw = [keep.tile([P, PACK, P], F32, name=f"h_raw{b}") for b in range(BLOCKS)]
+        h_first = keep.tile([P, PACK, P], F32)
+        h_second = keep.tile([P, PACK, P], F32)
+        h_rest = keep.tile([P, PACK, 2 * P], F32, tag="late")
+        h_raw = [h_first[:], h_second[:], h_rest[:, :, 0:P], h_rest[:, :, P : 2 * P]]
         h_view = hT.rearrange("(p j) t -> p j t", j=PACK)
 
         nc.gpsimd.memset(scale_rows[:].bitcast(I32), 0)
@@ -46,63 +50,85 @@ def tile_picked_ymochi_log_p_kernel(tc, x_words, x_scales, hT, share, inv, offs,
                 out=scale_rows[32 * q : 32 * q + 4, :].bitcast(I32),
                 in_=x_scales[0, 4 * q : 4 * q + 4, :].bitcast(I32),
             )
-        nc.sync.dma_start(out=h_raw[0][:], in_=h_view[:, :, 0:P])
         nc.sync.dma_start(out=words[:], in_=x_words[0].rearrange("p n t -> p (n t)").bitcast(I32))
-        nc.sync.dma_start(out=h_raw[1][:], in_=h_view[:, :, P : 2 * P])
+        nc.sync.dma_start(out=h_first[:], in_=h_view[:, :, 0:P])
         nc.sync.dma_start(share_sb[:], share)
         nc.sync.dma_start(inv_sb[:], inv)
         nc.sync.dma_start(one_sb[:], one)
         nc.sync.dma_start(two_sb[:], two)
-        for b in range(2, BLOCKS):
-            nc.sync.dma_start(out=h_raw[b][:], in_=h_view[:, :, b * P : (b + 1) * P])
+        nc.sync.dma_start(out=h_second[:], in_=h_view[:, :, P : 2 * P])
+        nc.sync.dma_start(out=h_rest[:], in_=h_view[:, :, 2 * P : 4 * P])
 
-        counts = keep.tile([P, BLOCKS, TERMS], F32)
-        horner = keep.tile([P, BLOCKS, TERMS + 1], F32)
-        exponent = keep.tile([P, 1], F32)
-        nc.gpsimd.iota(counts[:], pattern=[[0, BLOCKS], [-1, TERMS]], base=TERMS, channel_multiplier=0, allow_small_or_imprecise_dtypes=True)
-        nc.gpsimd.memset(exponent[:], -1.0 / ROOT)
-        nc.vector.tensor_scalar(counts[:], counts[:], -1.0 / ROOT, None, op0=ALU.mult)
-        nc.vector.reciprocal(horner[:, :, 0:TERMS], counts[:])
+        ones = keep.tile([P, 1], F32)
+        index = keep.tile([P, NODES], F32)
+        nodes = keep.tile([P, NODES], F32)
+        minus_nodes = keep.tile([P, NODES], F32)
+        log_step = keep.tile([P, 1], F32)
+        rule_at_one = keep.tile([P, 1], F32)
+        nc.gpsimd.memset(ones[:], 1.0)
+        nc.gpsimd.iota(index[:], pattern=[[1, NODES]], base=FIRST_NODE, channel_multiplier=0, allow_small_or_imprecise_dtypes=True)
+        nc.scalar.activation(log_step[:], ones[:], ACT.Copy, scale=math.log(STEP))
+        nc.scalar.activation(nodes[:], index[:], ACT.Exp, scale=STEP)
+        nc.scalar.activation(minus_nodes[:], nodes[:], ACT.Copy, scale=-1.0)
+        nc.scalar.activation(nodes[:], minus_nodes[:], ACT.Exp, bias=log_step[:], accum_out=rule_at_one[:])
 
         x_codes = keep.tile([P, S], U32, align_bytes=64)
         x_bytes = keep.tile([P, S], U8, align_bytes=64)
-        nc.vector.tensor_copy(x_bytes[:], scale_rows[:].indirect(offs_sb[:]))
-        nc.vector.tensor_copy(x_codes[:], words[:].bitcast(U32).indirect(offs_sb[:]))
+        last = BLOCKS - 1
+        halves = (slice(0, S // 2), slice(S // 2, S))
+        pieces = [(slice(0, S),) for b in range(BLOCKS)]
+        width = [W + len(pieces[b]) if b < last else S for b in range(BLOCKS)]
+        scores = [[psum.tile([P, cols.stop - cols.start], F32, name=f"scores{b}_{i}") for i, cols in enumerate(pieces[b])] for b in range(BLOCKS)]
+        logits = [keep.tile([P, width[b]], F32, name=f"logits{b}") for b in range(BLOCKS)]
+        total = [keep.tile([P, 1], F32, name=f"total{b}") for b in range(BLOCKS)]
+        minus_max = [keep.tile([P, 1], F32, name=f"minus_max{b}") for b in range(BLOCKS)]
+        rule = [keep.tile([P, 1], F32, name=f"rule{b}") for b in range(BLOCKS)]
+        minus_lse = [keep.tile([P, 1], F32, name=f"minus_lse{b}") for b in range(BLOCKS)]
+        h_codes = [keep.tile([P, P], U32, name=f"h_codes{b}", tag=f"codes{b}", align_bytes=64) for b in range(BLOCKS)]
+        h_bytes = [keep.tile([P, P], U8, name=f"h_bytes{b}", align_bytes=64) for b in range(BLOCKS)]
 
-        scores = []
-        for b in range(BLOCKS):
-            grouped = keep.tile([P, P, PACK], BF16, name=f"grouped{b}", align_bytes=64)
+        last_syn = keep.tile([P, R + 1], F32)
+        max_y = keep.tile([P, 1], F32)
+        minus_max_y = keep.tile([P, 1], F32)
+        shift_y = keep.tile([P, 1], F32)
+        total_y = keep.tile([P, 1], F32)
+        rule_y = keep.tile([P, 1], F32)
+        terms_y = keep.tile([P, NODES], F32)
+
+        def quantise(b):
+            grouped = keep.tile([P, P, PACK], BF16, name=f"grouped{b}", tag=f"grouped{b}", align_bytes=64)
             nc.scalar.activation(
                 grouped[:].rearrange("p (c i) j -> p c j i", i=4),
-                h_raw[b][:].rearrange("p j (c i) -> p c j i", i=4),
+                h_raw[b].rearrange("p j (c i) -> p c j i", i=4),
                 ACT.Copy,
             )
-            h_codes = keep.tile([P, P], U32, name=f"h_codes{b}", align_bytes=64)
-            h_bytes = keep.tile([P, P], U8, name=f"h_bytes{b}", align_bytes=64)
-            nc.vector.quantize_mx(out=h_codes[:].bitcast(FP8X4), scales=h_bytes[:], in_=grouped[:].rearrange("p t j -> p (t j)"))
-            acc = psum.tile([P, S], F32, name=f"acc{b}")
-            nc.tensor.matmul_mx(
-                out=acc[:], lhsT=h_codes[:].bitcast(FP8X4), lhsT_scale=h_bytes[:],
-                rhs=x_codes[:].bitcast(FP8X4), rhs_scale=x_bytes[:], start=True, stop=True,
-            )
-            scores.append(acc)
+            nc.vector.quantize_mx(out=h_codes[b][:].bitcast(FP8X4), scales=h_bytes[b][:], in_=grouped[:].rearrange("p t j -> p (t j)"))
 
-        weight_one = keep.tile([P, R], F32)
+        def multiply(b):
+            for i, cols in enumerate(pieces[b]):
+                nc.tensor.matmul_mx(
+                    out=scores[b][i][:], lhsT=h_codes[b][:].bitcast(FP8X4), lhsT_scale=h_bytes[b][:],
+                    rhs=x_codes[:, cols].bitcast(FP8X4), rhs_scale=x_bytes[:, cols], start=True, stop=True,
+                )
+
+        nc.vector.tensor_copy(x_bytes[:], scale_rows[:].indirect(offs_sb[:]))
+        nc.vector.tensor_copy(x_codes[:], words[:].bitcast(U32).indirect(offs_sb[:]))
+        quantise(0)
+        multiply(0)
+
+        weight_one = keep.tile([P, R], F32, tag="grouped0", align_bytes=64)
         weight_two = keep.tile([P, R], F32)
-        nc.vector.tensor_tensor(weight_one[:], share_sb[:], inv_sb[:], ALU.mult)
-        nc.vector.tensor_tensor(weight_two[:], inv_sb[:], weight_one[:], ALU.subtract)
-
-        logits = [keep.tile([P, W + 1], F32, name=f"logits{b}") for b in range(BLOCKS)]
-        part_one = [keep.tile([P, R], F32, name=f"part_one{b}") for b in range(BLOCKS)]
-        part_two = [keep.tile([P, R], F32, name=f"part_two{b}") for b in range(BLOCKS)]
-        result = [keep.tile([P, W], F32, name=f"result{b}") for b in range(BLOCKS)]
-        total = [keep.tile([P, 1], F32, name=f"total{b}") for b in range(BLOCKS)]
-        root = [keep.tile([P, 1], F32, name=f"root{b}") for b in range(BLOCKS)]
-        gap = [keep.tile([P, 1], F32, name=f"gap{b}") for b in range(BLOCKS)]
-        series = [keep.tile([P, TERMS + 1], F32, name=f"series{b}") for b in range(BLOCKS)]
 
         def leave_psum(b):
-            nc.vector.tensor_scalar(logits[b][:, 0:S], scores[b][:], 1.0, None, op0=ALU.mult, op1=ALU.max, accum_out=logits[b][:, W : W + 1])
+            for i, cols in enumerate(pieces[b]):
+                row_max = logits[b][:, W + i : W + i + 1] if b < last else max_y[:]
+                nc.vector.tensor_scalar(logits[b][:, cols], scores[b][i][:], 1.0, None, op0=ALU.mult, op1=ALU.max, accum_out=row_max)
+            if b == last:
+                nc.scalar.activation(minus_max_y[:], max_y[:], ACT.Copy, scale=-1.0)
+                nc.scalar.activation(shift_y[:], rule_at_one[:], ACT.Identity, bias=max_y[:])
+                nc.scalar.activation(result[b][:, 0:S], logits[b][:], ACT.Exp, bias=minus_max_y[:], accum_out=total_y[:])
+                nc.scalar.activation(terms_y[:], minus_nodes[:], ACT.Exp, scale=total_y[:], bias=log_step[:], accum_out=rule_y[:])
+                nc.scalar.activation(last_syn[:, R : R + 1], rule_y[:], ACT.Identity, scale=-1.0, bias=shift_y[:])
 
         def gather_one(b):
             nc.vector.tensor_tensor(part_one[b][:], logits[b][:].indirect(one_sb[:]), weight_one[:], ALU.mult)
@@ -111,34 +137,58 @@ def tile_picked_ymochi_log_p_kernel(tc, x_words, x_scales, hT, share, inv, offs,
             nc.vector.tensor_tensor(part_two[b][:], logits[b][:].indirect(two_sb[:]), weight_two[:], ALU.mult)
 
         def mix(b):
-            nc.vector.tensor_tensor(logits[b][:, S:W], part_one[b][:], part_two[b][:], ALU.add)
+            nc.vector.tensor_tensor(logits[b][:, S:W] if b < last else last_syn[:, 0:R], part_one[b][:], part_two[b][:], ALU.add)
 
-        def row_max(b):
-            nc.vector.tensor_reduce(horner[:, b, TERMS : TERMS + 1], logits[b][:, S : W + 1], axis=AXIS.X, op=ALU.max, negate=True)
-            nc.scalar.activation(result[b][:], logits[b][:, 0:W], ACT.Exp, bias=horner[:, b, TERMS : TERMS + 1], accum_out=total[b][:])
-            nc.gpsimd.tensor_tensor(root[b][:], total[b][:], exponent[:], ALU.pow)
-            nc.gpsimd.tensor_scalar(gap[b][:], root[b][:], -1.0, 1.0, op0=ALU.mult, op1=ALU.add)
+        def row_sum(b):
+            if b < last:
+                candidates, summed = logits[b][:, S : width[b]], logits[b][:, 0:W]
+                exps = logits[0][:, 0:W] if b == 2 else result[b][:, 0:W]
+                terms = result[b + 1][:, S : S + NODES]
+            else:
+                candidates, summed = last_syn[:], last_syn[:]
+                exps = result[b][:, S : W + 1]
+                terms = terms_y[:]
+            nc.vector.tensor_reduce(minus_max[b][:], candidates, axis=AXIS.X, op=ALU.max, negate=True)
+            nc.scalar.activation(exps, summed, ACT.Exp, bias=minus_max[b][:], accum_out=total[b][:])
+            nc.scalar.activation(shift[b], rule_at_one[:], ACT.Identity, scale=-1.0, bias=minus_max[b][:])
+            nc.scalar.activation(terms, minus_nodes[:], ACT.Exp, scale=total[b][:], bias=log_step[:], accum_out=rule[b][:])
 
         def finish(b):
-            nc.vector.tensor_tensor_scan(series[b][:], gap[b][:].to_broadcast([P, TERMS + 1]), horner[:, b, :], 0.0, op0=ALU.mult, op1=ALU.add)
-            minus_lse = series[b][:, TERMS : TERMS + 1]
-            if b < BLOCKS - 1:
-                nc.scalar.activation(result[b][:], logits[b][:, 0:W], ACT.Identity, bias=minus_lse)
+            rows = slice(b * P, (b + 1) * P)
+            if b == 0:
+                nc.scalar.activation(minus_lse[b][:], rule[b][:], ACT.Identity, bias=shift[b])
+                nc.scalar.activation(result[b][:, 0:W], logits[b][:, 0:W], ACT.Identity, bias=minus_lse[b][:])
+                nc.sync.dma_start(out=out[rows, :], in_=result[b][:, 0:W])
+            elif b < last:
+                nc.vector.tensor_scalar(result[b][:, 0:W], logits[b][:, 0:W], shift[b], rule[b][:], op0=ALU.add, op1=ALU.add)
+                nc.sync.dma_start(out=out[rows, :], in_=result[b][:, 0:W])
             else:
-                nc.vector.tensor_scalar(result[b][:, 0:S], logits[b][:, 0:S], minus_lse, None, op0=ALU.add)
-                nc.scalar.activation(result[b][:, S:W], logits[b][:, S:W], ACT.Identity, bias=minus_lse)
-            nc.sync.dma_start(out=out[b * P : (b + 1) * P, :], in_=result[b][:])
+                for queue, cols, source in ((nc.sync, slice(0, S), logits[b][:]), (nc.scalar, slice(S, W), last_syn[:, 0:R])):
+                    nc.vector.tensor_scalar(result[b][:, cols], source, shift[b], rule[b][:], op0=ALU.add, op1=ALU.add)
+                    queue.dma_start(out=out[rows, cols], in_=result[b][:, cols])
 
         leave_psum(0)
+        nc.vector.tensor_tensor(weight_one[:], share_sb[:], inv_sb[:], ALU.mult)
+        nc.vector.tensor_tensor(weight_two[:], inv_sb[:], weight_one[:], ALU.subtract)
+        for b in range(1, BLOCKS):
+            quantise(b)
+            multiply(b)
+        part_one = [keep.tile([P, R], F32, name=f"part_one{b}", tag=f"grouped{2 * b + 1}", align_bytes=64) for b in range(BLOCKS)]
+        part_two = [keep.tile([P, R], F32, name=f"part_two{b}", tag=f"codes{b + 1}", align_bytes=64) for b in range(BLOCKS)]
+        result = [keep.tile([P, W + 2], F32, name=f"result{b}", tag="late" if b == 0 else f"result{b}") for b in range(BLOCKS)]
+        shift = [result[b][:, W + 1 : W + 2] for b in range(BLOCKS)]
         gather_one(0)
         for b in range(BLOCKS):
             gather_two(b)
-            if b + 1 < BLOCKS:
+            if b < last:
                 leave_psum(b + 1)
             mix(b)
-            if b + 1 < BLOCKS:
+            if b < last:
                 gather_one(b + 1)
-            row_max(b)
-            if b > 0:
-                finish(b - 1)
-        finish(BLOCKS - 1)
+            else:
+                finish(1)
+            row_sum(b)
+            if b == 0:
+                finish(0)
+        finish(2)
+        finish(3)

import math
from contextlib import ExitStack

import concourse.mybir as mybir

K, T, S, V, R = 512, 1024, 512, 512, 256
P = 128
PACK = 4
BLOCKS = V // P
W = S + R
STEP = 0.4
FIRST_NODE, NODES = -71, 80
FLOPS = 2 * K * V * S

F32 = mybir.dt.float32
BF16 = mybir.dt.bfloat16
I32 = mybir.dt.int32
U32 = mybir.dt.uint32
U16 = mybir.dt.uint16
U8 = mybir.dt.uint8
FP8X4 = mybir.dt.float8_e4m3fn_x4
ALU = mybir.AluOpType
ACT = mybir.ActivationFunctionType
AXIS = mybir.AxisListType


def tile_picked_ymochi_log_p_kernel(tc, x_words, x_scales, hT, share, inv, offs, one, two, out):
    nc = tc.nc
    with ExitStack() as ctx:
        keep = ctx.enter_context(tc.tile_pool(name="keep", bufs=1))
        psum = ctx.enter_context(tc.psum_pool(name="psum", bufs=1))

        offs_sb = keep.tile([P, S // 16], U16)
        one_sb = keep.tile([P, R // 16], U16)
        two_sb = keep.tile([P, R // 16], U16)
        words = keep.tile([P, T], I32)
        scale_rows = keep.tile([P, T], U8)
        share_sb = keep.tile([P, R], F32)
        inv_sb = keep.tile([P, R], F32)
        h_first = keep.tile([P, PACK, P], F32)
        h_second = keep.tile([P, PACK, P], F32)
        h_rest = keep.tile([P, PACK, 2 * P], F32, tag="late")
        h_raw = [h_first[:], h_second[:], h_rest[:, :, 0:P], h_rest[:, :, P : 2 * P]]
        h_view = hT.rearrange("(p j) t -> p j t", j=PACK)

        nc.gpsimd.memset(scale_rows[:].bitcast(I32), 0)
        nc.sync.dma_start(offs_sb[:], offs)
        for q in range(4):
            nc.sync.dma_start(
                out=scale_rows[32 * q : 32 * q + 4, :].bitcast(I32),
                in_=x_scales[0, 4 * q : 4 * q + 4, :].bitcast(I32),
            )
        nc.sync.dma_start(out=words[:], in_=x_words[0].rearrange("p n t -> p (n t)").bitcast(I32))
        nc.sync.dma_start(out=h_first[:], in_=h_view[:, :, 0:P])
        nc.sync.dma_start(share_sb[:], share)
        nc.sync.dma_start(inv_sb[:], inv)
        nc.sync.dma_start(one_sb[:], one)
        nc.sync.dma_start(two_sb[:], two)
        nc.sync.dma_start(out=h_second[:], in_=h_view[:, :, P : 2 * P])
        nc.sync.dma_start(out=h_rest[:], in_=h_view[:, :, 2 * P : 4 * P])

        ones = keep.tile([P, 1], F32)
        index = keep.tile([P, NODES], F32)
        nodes = keep.tile([P, NODES], F32)
        minus_nodes = keep.tile([P, NODES], F32)
        log_step = keep.tile([P, 1], F32)
        rule_at_one = keep.tile([P, 1], F32)
        nc.gpsimd.memset(ones[:], 1.0)
        nc.gpsimd.iota(index[:], pattern=[[1, NODES]], base=FIRST_NODE, channel_multiplier=0, allow_small_or_imprecise_dtypes=True)
        nc.scalar.activation(log_step[:], ones[:], ACT.Copy, scale=math.log(STEP))
        nc.scalar.activation(nodes[:], index[:], ACT.Exp, scale=STEP)
        nc.scalar.activation(minus_nodes[:], nodes[:], ACT.Copy, scale=-1.0)
        nc.scalar.activation(nodes[:], minus_nodes[:], ACT.Exp, bias=log_step[:], accum_out=rule_at_one[:])

        x_codes = keep.tile([P, S], U32, align_bytes=64)
        x_bytes = keep.tile([P, S], U8, align_bytes=64)
        last = BLOCKS - 1
        halves = (slice(0, S // 2), slice(S // 2, S))
        pieces = [(slice(0, S),) for b in range(BLOCKS)]
        width = [W + len(pieces[b]) if b < last else S for b in range(BLOCKS)]
        scores = [[psum.tile([P, cols.stop - cols.start], F32, name=f"scores{b}_{i}") for i, cols in enumerate(pieces[b])] for b in range(BLOCKS)]
        logits = [keep.tile([P, width[b]], F32, name=f"logits{b}") for b in range(BLOCKS)]
        total = [keep.tile([P, 1], F32, name=f"total{b}") for b in range(BLOCKS)]
        minus_max = [keep.tile([P, 1], F32, name=f"minus_max{b}") for b in range(BLOCKS)]
        rule = [keep.tile([P, 1], F32, name=f"rule{b}") for b in range(BLOCKS)]
        minus_lse = [keep.tile([P, 1], F32, name=f"minus_lse{b}") for b in range(BLOCKS)]
        h_codes = [keep.tile([P, P], U32, name=f"h_codes{b}", tag=f"codes{b}", align_bytes=64) for b in range(BLOCKS)]
        h_bytes = [keep.tile([P, P], U8, name=f"h_bytes{b}", align_bytes=64) for b in range(BLOCKS)]

        last_syn = keep.tile([P, R + 1], F32)
        max_y = keep.tile([P, 1], F32)
        minus_max_y = keep.tile([P, 1], F32)
        shift_y = keep.tile([P, 1], F32)
        total_y = keep.tile([P, 1], F32)
        rule_y = keep.tile([P, 1], F32)
        terms_y = keep.tile([P, NODES], F32)

        def quantise(b):
            grouped = keep.tile([P, P, PACK], BF16, name=f"grouped{b}", tag=f"grouped{b}", align_bytes=64)
            nc.scalar.activation(
                grouped[:].rearrange("p (c i) j -> p c j i", i=4),
                h_raw[b].rearrange("p j (c i) -> p c j i", i=4),
                ACT.Copy,
            )
            nc.vector.quantize_mx(out=h_codes[b][:].bitcast(FP8X4), scales=h_bytes[b][:], in_=grouped[:].rearrange("p t j -> p (t j)"))

        def multiply(b):
            for i, cols in enumerate(pieces[b]):
                nc.tensor.matmul_mx(
                    out=scores[b][i][:], lhsT=h_codes[b][:].bitcast(FP8X4), lhsT_scale=h_bytes[b][:],
                    rhs=x_codes[:, cols].bitcast(FP8X4), rhs_scale=x_bytes[:, cols], start=True, stop=True,
                )

        nc.vector.tensor_copy(x_bytes[:], scale_rows[:].indirect(offs_sb[:]))
        nc.vector.tensor_copy(x_codes[:], words[:].bitcast(U32).indirect(offs_sb[:]))
        quantise(0)
        multiply(0)

        weight_one = keep.tile([P, R], F32, tag="grouped0", align_bytes=64)
        weight_two = keep.tile([P, R], F32)

        def leave_psum(b):
            for i, cols in enumerate(pieces[b]):
                row_max = logits[b][:, W + i : W + i + 1] if b < last else max_y[:]
                nc.vector.tensor_scalar(logits[b][:, cols], scores[b][i][:], 1.0, None, op0=ALU.mult, op1=ALU.max, accum_out=row_max)
            if b == last:
                nc.scalar.activation(minus_max_y[:], max_y[:], ACT.Copy, scale=-1.0)
                nc.scalar.activation(shift_y[:], rule_at_one[:], ACT.Identity, bias=max_y[:])
                nc.scalar.activation(result[b][:, 0:S], logits[b][:], ACT.Exp, bias=minus_max_y[:], accum_out=total_y[:])
                nc.scalar.activation(terms_y[:], minus_nodes[:], ACT.Exp, scale=total_y[:], bias=log_step[:], accum_out=rule_y[:])
                nc.scalar.activation(last_syn[:, R : R + 1], rule_y[:], ACT.Identity, scale=-1.0, bias=shift_y[:])

        def gather_one(b):
            nc.vector.tensor_tensor(part_one[b][:], logits[b][:].indirect(one_sb[:]), weight_one[:], ALU.mult)

        def gather_two(b):
            nc.vector.tensor_tensor(part_two[b][:], logits[b][:].indirect(two_sb[:]), weight_two[:], ALU.mult)

        def mix(b):
            nc.vector.tensor_tensor(logits[b][:, S:W] if b < last else last_syn[:, 0:R], part_one[b][:], part_two[b][:], ALU.add)

        def row_sum(b):
            if b < last:
                candidates, summed = logits[b][:, S : width[b]], logits[b][:, 0:W]
                exps = logits[0][:, 0:W] if b == 2 else result[b][:, 0:W]
                terms = result[b + 1][:, S : S + NODES]
            else:
                candidates, summed = last_syn[:], last_syn[:]
                exps = result[b][:, S : W + 1]
                terms = terms_y[:]
            nc.vector.tensor_reduce(minus_max[b][:], candidates, axis=AXIS.X, op=ALU.max, negate=True)
            nc.scalar.activation(exps, summed, ACT.Exp, bias=minus_max[b][:], accum_out=total[b][:])
            nc.scalar.activation(shift[b], rule_at_one[:], ACT.Identity, scale=-1.0, bias=minus_max[b][:])
            nc.scalar.activation(terms, minus_nodes[:], ACT.Exp, scale=total[b][:], bias=log_step[:], accum_out=rule[b][:])

        def finish(b):
            rows = slice(b * P, (b + 1) * P)
            if b == 0:
                nc.scalar.activation(minus_lse[b][:], rule[b][:], ACT.Identity, bias=shift[b])
                nc.scalar.activation(result[b][:, 0:W], logits[b][:, 0:W], ACT.Identity, bias=minus_lse[b][:])
                nc.sync.dma_start(out=out[rows, :], in_=result[b][:, 0:W])
            elif b < last:
                nc.vector.tensor_scalar(result[b][:, 0:W], logits[b][:, 0:W], shift[b], rule[b][:], op0=ALU.add, op1=ALU.add)
                nc.sync.dma_start(out=out[rows, :], in_=result[b][:, 0:W])
            else:
                for queue, cols, source in ((nc.sync, slice(0, S), logits[b][:]), (nc.scalar, slice(S, W), last_syn[:, 0:R])):
                    nc.vector.tensor_scalar(result[b][:, cols], source, shift[b], rule[b][:], op0=ALU.add, op1=ALU.add)
                    queue.dma_start(out=out[rows, cols], in_=result[b][:, cols])

        leave_psum(0)
        nc.vector.tensor_tensor(weight_one[:], share_sb[:], inv_sb[:], ALU.mult)
        nc.vector.tensor_tensor(weight_two[:], inv_sb[:], weight_one[:], ALU.subtract)
        for b in range(1, BLOCKS):
            quantise(b)
            multiply(b)
        part_one = [keep.tile([P, R], F32, name=f"part_one{b}", tag=f"grouped{2 * b + 1}", align_bytes=64) for b in range(BLOCKS)]
        part_two = [keep.tile([P, R], F32, name=f"part_two{b}", tag=f"codes{b + 1}", align_bytes=64) for b in range(BLOCKS)]
        result = [keep.tile([P, W + 2], F32, name=f"result{b}", tag="late" if b == 0 else f"result{b}") for b in range(BLOCKS)]
        shift = [result[b][:, W + 1 : W + 2] for b in range(BLOCKS)]
        gather_one(0)
        for b in range(BLOCKS):
            gather_two(b)
            if b < last:
                leave_psum(b + 1)
            mix(b)
            if b < last:
                gather_one(b + 1)
            else:
                finish(1)
            row_sum(b)
            if b == 0:
                finish(0)
        finish(2)
        finish(3)
